import numpy as np
CORES = [3,0,2,1,6,7,4,5]
N = 8
GROUPS = [[0,2,4,6],[1,3,5,7]]
def setup_inputs(rng):
    return {"x": rng.standard_normal((N, 128, 8), dtype=np.float32)}
def reference(x):
    y = np.empty((N, 128, 8), x.dtype)
    for g in GROUPS:
        n = len(g); b = x.shape[2] // n
        for i, r in enumerate(g):
            y[r] = np.concatenate([x[s][:, i * b:(i + 1) * b] for s in g], axis=1)
    return {"y": y}

from concourse.bass import DstId, RemoteDMATransfer

SCRATCH = {
    "send": ("sbuf", [128, 8], "float32"),
    "land": ("sbuf", [128, 8], "float32"),
}
SEMAPHORES = ["loaded", "read", "arrived", "stored"]

ENG = 4


def rank_program(g, core, T, topo):
    rank = T.rank_of(core)
    if rank is None:
        return
    group = [grp for grp in T.tables["GROUPS"] if rank in grp][0]
    n = len(group)
    me = group.index(rank)
    b = T.x.shape[1] // n

    def blk(k):
        return slice(k * b, (k + 1) * b)

    g.dma_start(T.send[:], T.x[:]).then_inc(T.sem.loaded, 16)
    g.dma_start(T.land[:, blk(me)], T.x[:, blk(me)]).then_inc(T.sem.loaded, 16)
    g.wait_ge(T.sem.loaded, 32)

    transfers = []
    for j, r in enumerate(group):
        if j == me:
            continue
        rid, pid = topo.addr(T.cores[r])[:2]
        lane = len(transfers)
        transfers.append(RemoteDMATransfer(
            dst_ids=[DstId(rid=rid, pnc=pid)],
            dma_engine_mask=((1 << ENG) - 1) << (ENG * lane),
            remote_sem=T.sem.arrived,
            src=T.send[:, blk(j)],
            dst=T.land[:, blk(me)],
        ))
    g.remote_dma_fused(transfers, local_sem=T.sem.read)

    g.wait_ge(T.sem.arrived, ENG * (n - 1))
    g.wait_ge(T.sem.read, ENG * (n - 1))

    g.dma_start(T.y[:], T.land[:]).then_inc(T.sem.stored, 16)
    g.wait_ge(T.sem.stored, 16)
